import numpy as np
import ml_dtypes

BF16 = ml_dtypes.bfloat16


def bf(x):
    return np.asarray(x, np.float32).astype(BF16)


def f32(x):
    return np.asarray(x, np.float32)


def f64(x):
    return np.asarray(x).astype(np.float64)


def striped(idx):
    return np.tile(idx.reshape(-1, 16).T, (8, 1))


S, K, M, N, E, Q, V, D = 512, 256, 512, 256, 1, 256, 256, 2


def setup_inputs():
    return {"base": bf(np.random.standard_normal((M, S))), "x": bf(np.random.standard_normal((K, N))), "w": bf(1.5 * np.random.standard_normal((E, K, M)) / np.sqrt(K)), "offs": striped(np.random.permutation(S)[:N])}


def reference(base, x, w, offs):
    idx = offs[:16].T.reshape(-1)
    z = f64(base).copy()
    for e in range(E):
        z[:, idx[e * Q : (e + 1) * Q]] += f64(w)[e].T @ f64(x)[:, e * Q : (e + 1) * Q]
    z = z
    return z.reshape(M, V, D).max(axis=2)

@@ -1,0 +1,55 @@
+import concourse.mybir as mybir
+from concourse.masks import make_identity
+
+BF16, F32, U16 = mybir.dt.bfloat16, mybir.dt.float32, mybir.dt.uint16
+P = 128
+FLOPS = 2 * 256 * 512 * 256
+
+
+def tile_rows_unpool_max_none_kernel(tc, base, x, w, offs, out):
+    nc = tc.nc
+    features, cells = base.shape
+    depth, points = x.shape
+    pool_by = cells // out.shape[1]
+    blocks, ksteps = features // P, depth // P
+
+    with (
+        tc.tile_pool(name="held", bufs=1) as held,
+        tc.psum_pool(name="psum", bufs=1) as psum,
+    ):
+        grids = [held.tile([P, cells], BF16, name=f"grid{m}") for m in range(blocks)]
+        for m in range(blocks):
+            nc.sync.dma_start(grids[m][:], base[m * P : (m + 1) * P, :])
+        weights = held.tile([P, ksteps, features], BF16, name="weights")
+        nc.sync.dma_start(weights[:], w[0].rearrange("(k p) m -> p k m", p=P))
+        moving = held.tile([P, ksteps, points], BF16, name="moving")
+        nc.sync.dma_start(moving[:], x.rearrange("(k p) j -> p k j", p=P))
+        offsets = held.tile([P, points // 16], U16, name="offsets")
+        nc.sync.dma_start(offsets[:], offs)
+
+        identity = held.tile([P, P], BF16, name="identity")
+        make_identity(nc, identity[:])
+
+        windows = [psum.tile([P, cells], F32, name=f"window{m}") for m in range(blocks)]
+        for m in range(blocks):
+            nc.tensor.matmul(windows[m][:], identity[:], grids[m][:], start=True, stop=False)
+
+        for m in range(blocks):
+            for k in range(ksteps):
+                nc.tensor.matmul(
+                    windows[m][:].indirect(offsets[:]),
+                    weights[:, k, m * P : (m + 1) * P],
+                    moving[:, k, :],
+                    start=False,
+                    stop=k == ksteps - 1,
+                )
+
+        for m in range(blocks):
+            pooled = held.tile([P, cells // pool_by], F32, name=f"pooled{m}")
+            nc.vector.tensor_reduce(
+                pooled[:],
+                windows[m][:].rearrange("p (v d) -> p v d", d=pool_by),
+                mybir.AxisListType.X,
+                mybir.AluOpType.max,
+            )
+            nc.sync.dma_start(out[m * P : (m + 1) * P, :], pooled[:])

@@ -3,6 +3,7 @@ from concourse.masks import make_identity
 
 BF16, F32, U16 = mybir.dt.bfloat16, mybir.dt.float32, mybir.dt.uint16
 P = 128
+WARMUPS = 12
 FLOPS = 2 * 256 * 512 * 256
 
 
@@ -17,6 +18,12 @@ def tile_rows_unpool_max_none_kernel(tc, base, x, w, offs, out):
         tc.tile_pool(name="held", bufs=1) as held,
         tc.psum_pool(name="psum", bufs=1) as psum,
     ):
+        zeros = held.tile([P, P], BF16, name="zeros")
+        nc.vector.memset(zeros[:], 0.0)
+        spare = psum.tile([P, P], F32, name="spare")
+        for i in range(WARMUPS):
+            nc.tensor.matmul(spare[:], zeros[:], zeros[:], start=True, stop=True)
+
         grids = [held.tile([P, cells], BF16, name=f"grid{m}") for m in range(blocks)]
         for m in range(blocks):
             nc.sync.dma_start(grids[m][:], base[m * P : (m + 1) * P, :])

import concourse.mybir as mybir
from concourse.masks import make_identity

BF16, F32, U16 = mybir.dt.bfloat16, mybir.dt.float32, mybir.dt.uint16
P = 128
WARMUPS = 12
FLOPS = 2 * 256 * 512 * 256


def tile_rows_unpool_max_none_kernel(tc, base, x, w, offs, out):
    nc = tc.nc
    features, cells = base.shape
    depth, points = x.shape
    pool_by = cells // out.shape[1]
    blocks, ksteps = features // P, depth // P

    with (
        tc.tile_pool(name="held", bufs=1) as held,
        tc.psum_pool(name="psum", bufs=1) as psum,
    ):
        zeros = held.tile([P, P], BF16, name="zeros")
        nc.vector.memset(zeros[:], 0.0)
        spare = psum.tile([P, P], F32, name="spare")
        for i in range(WARMUPS):
            nc.tensor.matmul(spare[:], zeros[:], zeros[:], start=True, stop=True)

        grids = [held.tile([P, cells], BF16, name=f"grid{m}") for m in range(blocks)]
        for m in range(blocks):
            nc.sync.dma_start(grids[m][:], base[m * P : (m + 1) * P, :])
        weights = held.tile([P, ksteps, features], BF16, name="weights")
        nc.sync.dma_start(weights[:], w[0].rearrange("(k p) m -> p k m", p=P))
        moving = held.tile([P, ksteps, points], BF16, name="moving")
        nc.sync.dma_start(moving[:], x.rearrange("(k p) j -> p k j", p=P))
        offsets = held.tile([P, points // 16], U16, name="offsets")
        nc.sync.dma_start(offsets[:], offs)

        identity = held.tile([P, P], BF16, name="identity")
        make_identity(nc, identity[:])

        windows = [psum.tile([P, cells], F32, name=f"window{m}") for m in range(blocks)]
        for m in range(blocks):
            nc.tensor.matmul(windows[m][:], identity[:], grids[m][:], start=True, stop=False)

        for m in range(blocks):
            for k in range(ksteps):
                nc.tensor.matmul(
                    windows[m][:].indirect(offsets[:]),
                    weights[:, k, m * P : (m + 1) * P],
                    moving[:, k, :],
                    start=False,
                    stop=k == ksteps - 1,
                )

        for m in range(blocks):
            pooled = held.tile([P, cells // pool_by], F32, name=f"pooled{m}")
            nc.vector.tensor_reduce(
                pooled[:],
                windows[m][:].rearrange("p (v d) -> p v d", d=pool_by),
                mybir.AxisListType.X,
                mybir.AluOpType.max,
            )
            nc.sync.dma_start(out[m * P : (m + 1) * P, :], pooled[:])
